import numpy as np
import ml_dtypes


def mxq(x, axis, fmt="e4m3"):
    dtype, down = {"e4m3": (ml_dtypes.float8_e4m3fn, 7), "e5m2": (ml_dtypes.float8_e5m2, 14)}[fmt]
    v = np.moveaxis(np.asarray(x, np.float32).astype(ml_dtypes.bfloat16).astype(np.float64), axis, -1)
    blocks = v.reshape(v.shape[:-1] + (-1, 32))
    amax = np.abs(blocks).max(-1, keepdims=True)
    byte = np.maximum(np.where(amax > 0, np.frexp(amax)[1] - 1 + 127, 0) - down, 1)
    scale = np.exp2(byte - 127.0)
    codes = (blocks / scale).astype(np.float32).astype(dtype).astype(np.float64)
    return np.moveaxis((codes * scale).reshape(v.shape), -1, axis)


WIDE = False


def mx_kscale(k):
    if not WIDE:
        return np.ones(k)
    levels = np.array([10, -10, 5, -5, 0])
    if k % 512:
        return np.exp2(np.random.permutation(np.resize(levels, k // 32))).repeat(32)
    a = np.empty((k // 512, 16))
    for p in range(k // 512):
        a[p, :8] = np.random.permutation(np.resize(levels, 8))
        for g in range(8):
            far = levels[np.abs(levels - a[p, g]) >= 10]
            a[p, g + 8] = far[np.random.randint(len(far))]
    return np.exp2(a.ravel()).repeat(32)


def f64(x):
    return np.asarray(x).astype(np.float64)


def striped(idx):
    return np.tile(np.asarray(idx).reshape(-1, 16).T, (8, 1)).astype(np.uint16)


def unstriped(offs):
    return offs[:16].T.reshape(-1).astype(np.int64)


G, K, T, D, M = 512, 4, 2048, 512, 256


def setup_inputs():
    n = np.random.standard_normal
    s = mx_kscale(D)[:, None]
    grid = lambda x: np.round(x * 32) / 32
    x = grid(n((D, T))) * s
    idx = np.random.randint(0, T, (G, K))
    return {
        "xT": x.astype(np.float32),
        "w": (n((D, M)) / np.sqrt(D * K) / s).astype(np.float32),
        "offs": striped(idx.reshape(-1)),
    }


def reference(xT, w, offs):
    x = f64(xT)[:, unstriped(offs)]
    y = mxq(f64(w), 0, "e4m3").T @ mxq(x.reshape(D, G, K).sum(-1), 0, "e4m3")
    return y

@@ -1,0 +1,128 @@
+from contextlib import ExitStack
+
+import concourse.mybir as mybir
+
+D, T, G, K, M = 512, 2048, 512, 4, 256
+P = 128
+FLOPS = 2 * D * G * M
+
+F32 = mybir.dt.float32
+BF16 = mybir.dt.bfloat16
+U32 = mybir.dt.uint32
+U16 = mybir.dt.uint16
+U8 = mybir.dt.uint8
+FP8X4 = mybir.dt.float8_e4m3fn_x4
+ADD = mybir.AluOpType.add
+COPY = mybir.ActivationFunctionType.Copy
+
+LOAD = 512
+BAGS = (128, 128, 128, 128)
+VECTOR_COLS = {(0, 3): 352, (1, 3): 160}
+GPSIMD_L1 = {(0, 0), (0, 1), (0, 2), (0, 3), (1, 0), (1, 1), (1, 2)}
+
+
+def tile_attend_bag_kernel(tc, xT, w, offs, out):
+    nc = tc.nc
+    x_rows = xT.rearrange("(p t) c -> p t c", t=4)
+    w_rows = w.rearrange("(p t) m -> p t m", t=4)
+    with ExitStack() as ctx:
+        keep = ctx.enter_context(tc.tile_pool(name="keep", bufs=1))
+        psum = ctx.enter_context(tc.psum_pool(name="psum", bufs=1))
+
+        offsets = keep.tile([P, G * K // 16], U16, name="offsets")
+        pairs = [keep.tile([P, 2 * T], BF16, name=f"pair{h}") for h in range(2)]
+
+        warm = keep.tile([P, 1], F32, name="warm")
+        warmed = keep.tile([P, 1], F32, name="warmed")
+        nc.vector.memset(warm[:], 0.0)
+        nc.scalar.activation(warmed[:], warm[:], COPY)
+
+        raws = {}
+        for h in range(2):
+            for k in range(T // LOAD):
+                raw = keep.tile([P, 2, LOAD], F32, name=f"raw{h}_{k}")
+                nc.sync.dma_start(raw[:], x_rows[:, 2 * h : 2 * h + 2, k * LOAD : (k + 1) * LOAD])
+                raws[h, k] = raw
+                if (h, k) == (0, 0):
+                    nc.sync.dma_start(offsets[:], offs)
+        w_raw = keep.tile([P, 4, M], F32, name="w_raw")
+        nc.sync.dma_start(w_raw[:], w_rows)
+
+        def cast(h, k):
+            wide = pairs[h][:].rearrange("p (c t) -> p c t", t=2)
+            raw = raws[h, k][:].rearrange("p t c -> p c t")
+            split = LOAD - VECTOR_COLS.get((h, k), 0)
+            c0 = k * LOAD
+            nc.scalar.activation(wide[:, c0 : c0 + split, :], raw[:, 0:split, :], COPY)
+            if split < LOAD:
+                nc.vector.tensor_copy(wide[:, c0 + split : c0 + LOAD, :], raw[:, split:LOAD, :])
+
+        sums = []
+        for i, bags in enumerate(BAGS):
+            s = keep.tile([P, 2, bags, 4], F32, name=f"sums{i}")
+            sums.append(s)
+        got = {}
+        starts = [sum(BAGS[:i]) for i in range(len(BAGS))]
+
+        def gather(h, i):
+            a = starts[i] * K // 16
+            b = a + BAGS[i] * K // 16
+            g = keep.tile([P, BAGS[i] * K], U32, name=f"got{h}_{i}")
+            nc.vector.tensor_copy(g[:], pairs[h][:].bitcast(U32).indirect(offsets[:, a:b]))
+            got[h, i] = g
+
+        def level1(h, i):
+            v = got[h, i][:].bitcast(BF16).rearrange("p (g e) -> p g e", e=8)
+            engine = nc.gpsimd if (h, i) in GPSIMD_L1 else nc.vector
+            engine.tensor_tensor(sums[i][:, h, :, :], v[:, :, 0:4], v[:, :, 4:8], ADD)
+
+        for k in range(T // LOAD):
+            cast(0, k)
+        for i in range(len(BAGS)):
+            gather(0, i)
+            level1(0, i)
+        for k in range(T // LOAD):
+            cast(1, k)
+        w_bf = keep.tile([P, M * 4], BF16, name="w_bf", align_bytes=64)
+        nc.scalar.activation(w_bf[:].rearrange("p (m t) -> p m t", t=4), w_raw[:].rearrange("p t m -> p m t"), COPY)
+        for i in range(len(BAGS)):
+            gather(1, i)
+            level1(1, i)
+
+        w_codes = keep.tile([P, M], U32, name="w_codes", align_bytes=64)
+        w_scales = keep.tile([P, M], U8, name="w_scales", align_bytes=64)
+        nc.vector.quantize_mx(w_codes[:].bitcast(FP8X4), w_scales[:], w_bf[:])
+
+        e_bf = []
+        for i, bags in enumerate(BAGS):
+            e = keep.tile([P, bags * 4], BF16, name=f"e{i}", align_bytes=64)
+            nc.vector.tensor_tensor(
+                e[:].rearrange("p (g h t) -> p g h t", h=2, t=2),
+                sums[i][:, :, :, 0:2].rearrange("p h g t -> p g h t"),
+                sums[i][:, :, :, 2:4].rearrange("p h g t -> p g h t"),
+                ADD,
+            )
+            e_bf.append(e)
+
+        for i, bags in enumerate(BAGS):
+            codes = keep.tile([P, bags], U32, name=f"codes{i}", align_bytes=64)
+            scales = keep.tile([P, bags], U8, name=f"scales{i}", align_bytes=64)
+            nc.vector.quantize_mx(codes[:].bitcast(FP8X4), scales[:], e_bf[i][:])
+            for m in range(2):
+                acc = psum.tile([P, bags], F32, name=f"acc{i}_{m}")
+                cols = slice(m * P, (m + 1) * P)
+                nc.tensor.matmul_mx(
+                    acc[:],
+                    lhsT=w_codes[:, cols].bitcast(FP8X4),
+                    lhsT_scale=w_scales[:, cols],
+                    rhs=codes[:].bitcast(FP8X4),
+                    rhs_scale=scales[:],
+                    start=True,
+                    stop=True,
+                )
+                res = keep.tile([P, bags], F32, name=f"res{i}_{m}")
+                if m == 1 and i == len(BAGS) - 1:
+                    nc.vector.tensor_copy(res[:], acc[:])
+                else:
+                    nc.scalar.activation(res[:], acc[:], COPY)
+                nc.sync.dma_start(out[cols, starts[i] : starts[i] + bags], res[:])

@@ -14,17 +14,21 @@ U8 = mybir.dt.uint8
 FP8X4 = mybir.dt.float8_e4m3fn_x4
 ADD = mybir.AluOpType.add
 COPY = mybir.ActivationFunctionType.Copy
+X = mybir.AxisListType.X
 
-LOAD = 512
+LOADS = ((512, 512, 768, 256), (512, 512, 512, 256, 256))
+VECTOR_COLS = {(0, 2): 512, (0, 3): 160}
 BAGS = (128, 128, 128, 128)
-VECTOR_COLS = {(0, 3): 352, (1, 3): 160}
-GPSIMD_L1 = {(0, 0), (0, 1), (0, 2), (0, 3), (1, 0), (1, 1), (1, 2)}
+GPSIMD = {(0, 0), (0, 1), (0, 2), (0, 3), (1, 0), (1, 1)}
+REDUCED = ()
 
 
 def tile_attend_bag_kernel(tc, xT, w, offs, out):
     nc = tc.nc
     x_rows = xT.rearrange("(p t) c -> p t c", t=4)
     w_rows = w.rearrange("(p t) m -> p t m", t=4)
+    out_rows = out.rearrange("(m p) g -> p m g", m=2)
+    starts = [sum(BAGS[:i]) for i in range(len(BAGS))]
     with ExitStack() as ctx:
         keep = ctx.enter_context(tc.tile_pool(name="keep", bufs=1))
         psum = ctx.enter_context(tc.psum_pool(name="psum", bufs=1))
@@ -32,37 +36,44 @@ def tile_attend_bag_kernel(tc, xT, w, offs, out):
         offsets = keep.tile([P, G * K // 16], U16, name="offsets")
         pairs = [keep.tile([P, 2 * T], BF16, name=f"pair{h}") for h in range(2)]
 
+        raws = {}
+        for h in range(2):
+            c = 0
+            for k, cols in enumerate(LOADS[h]):
+                raw = keep.tile([P, 2, cols], F32, name=f"raw{h}_{k}")
+                nc.sync.dma_start(raw[:], x_rows[:, 2 * h : 2 * h + 2, c : c + cols])
+                raws[h, k] = (raw, c)
+                c += cols
+                if (h, k) == (0, 3):
+                    nc.sync.dma_start(offsets[:], offs)
+        w_raw = keep.tile([P, 4, M], F32, name="w_raw")
+        nc.sync.dma_start(w_raw[:], w_rows)
+
         warm = keep.tile([P, 1], F32, name="warm")
         warmed = keep.tile([P, 1], F32, name="warmed")
         nc.vector.memset(warm[:], 0.0)
         nc.scalar.activation(warmed[:], warm[:], COPY)
 
-        raws = {}
-        for h in range(2):
-            for k in range(T // LOAD):
-                raw = keep.tile([P, 2, LOAD], F32, name=f"raw{h}_{k}")
-                nc.sync.dma_start(raw[:], x_rows[:, 2 * h : 2 * h + 2, k * LOAD : (k + 1) * LOAD])
-                raws[h, k] = raw
-                if (h, k) == (0, 0):
-                    nc.sync.dma_start(offsets[:], offs)
-        w_raw = keep.tile([P, 4, M], F32, name="w_raw")
-        nc.sync.dma_start(w_raw[:], w_rows)
-
         def cast(h, k):
+            tile, c0 = raws[h, k]
+            cols = LOADS[h][k]
             wide = pairs[h][:].rearrange("p (c t) -> p c t", t=2)
-            raw = raws[h, k][:].rearrange("p t c -> p c t")
-            split = LOAD - VECTOR_COLS.get((h, k), 0)
-            c0 = k * LOAD
-            nc.scalar.activation(wide[:, c0 : c0 + split, :], raw[:, 0:split, :], COPY)
-            if split < LOAD:
-                nc.vector.tensor_copy(wide[:, c0 + split : c0 + LOAD, :], raw[:, split:LOAD, :])
+            raw = tile[:].rearrange("p t c -> p c t")
+            split = cols - VECTOR_COLS.get((h, k), 0)
+            if split:
+                nc.scalar.activation(wide[:, c0 : c0 + split, :], raw[:, 0:split, :], COPY)
+            if split < cols:
+                nc.vector.tensor_copy(wide[:, c0 + split : c0 + cols, :], raw[:, split:cols, :])
 
-        sums = []
+        sums = {}
+        e_bf = []
         for i, bags in enumerate(BAGS):
-            s = keep.tile([P, 2, bags, 4], F32, name=f"sums{i}")
-            sums.append(s)
+            if i not in REDUCED:
+                s = keep.tile([P, 2, bags, 4], F32, name=f"sums{i}")
+                sums[i] = s
+            e = keep.tile([P, bags * 4], BF16, name=f"e{i}", align_bytes=64)
+            e_bf.append(e)
         got = {}
-        starts = [sum(BAGS[:i]) for i in range(len(BAGS))]
 
         def gather(h, i):
             a = starts[i] * K // 16
@@ -73,46 +84,51 @@ def tile_attend_bag_kernel(tc, xT, w, offs, out):
 
         def level1(h, i):
             v = got[h, i][:].bitcast(BF16).rearrange("p (g e) -> p g e", e=8)
-            engine = nc.gpsimd if (h, i) in GPSIMD_L1 else nc.vector
+            engine = nc.gpsimd if (h, i) in GPSIMD else nc.vector
             engine.tensor_tensor(sums[i][:, h, :, :], v[:, :, 0:4], v[:, :, 4:8], ADD)
 
-        for k in range(T // LOAD):
-            cast(0, k)
-        for i in range(len(BAGS)):
-            gather(0, i)
-            level1(0, i)
-        for k in range(T // LOAD):
-            cast(1, k)
-        w_bf = keep.tile([P, M * 4], BF16, name="w_bf", align_bytes=64)
-        nc.scalar.activation(w_bf[:].rearrange("p (m t) -> p m t", t=4), w_raw[:].rearrange("p t m -> p m t"), COPY)
-        for i in range(len(BAGS)):
-            gather(1, i)
-            level1(1, i)
-
-        w_codes = keep.tile([P, M], U32, name="w_codes", align_bytes=64)
-        w_scales = keep.tile([P, M], U8, name="w_scales", align_bytes=64)
-        nc.vector.quantize_mx(w_codes[:].bitcast(FP8X4), w_scales[:], w_bf[:])
-
-        e_bf = []
-        for i, bags in enumerate(BAGS):
-            e = keep.tile([P, bags * 4], BF16, name=f"e{i}", align_bytes=64)
+        def level2(i):
             nc.vector.tensor_tensor(
-                e[:].rearrange("p (g h t) -> p g h t", h=2, t=2),
+                e_bf[i][:].rearrange("p (g h t) -> p g h t", h=2, t=2),
                 sums[i][:, :, :, 0:2].rearrange("p h g t -> p g h t"),
                 sums[i][:, :, :, 2:4].rearrange("p h g t -> p g h t"),
                 ADD,
             )
-            e_bf.append(e)
 
-        for i, bags in enumerate(BAGS):
+        def reduce(h, i):
+            with nc.allow_low_precision(reason="the engine adds in float32 and rounds the sum once"):
+                nc.vector.tensor_reduce(
+                    e_bf[i][:].rearrange("p (g h t) -> p g h t", h=2, t=2)[:, :, h, :],
+                    got[h, i][:].bitcast(BF16).rearrange("p (g j t) -> p g t j", j=4, t=2),
+                    axis=X,
+                    op=ADD,
+                )
+
+        w_bf = keep.tile([P, M * 4], BF16, name="w_bf", align_bytes=64)
+        w_codes = keep.tile([P, M], U32, name="w_codes", align_bytes=64)
+        w_scales = keep.tile([P, M], U8, name="w_scales", align_bytes=64)
+
+        def quantise_w():
+            nc.vector.quantize_mx(w_codes[:].bitcast(FP8X4), w_scales[:], w_bf[:])
+
+        def product(i, last=False):
+            bags = BAGS[i]
             codes = keep.tile([P, bags], U32, name=f"codes{i}", align_bytes=64)
             scales = keep.tile([P, bags], U8, name=f"scales{i}", align_bytes=64)
             nc.vector.quantize_mx(codes[:].bitcast(FP8X4), scales[:], e_bf[i][:])
+            res = keep.tile([P, 2, bags], F32, name=f"res{i}")
+            accs = []
+            if last or bags > 256:
+                for m in range(2):
+                    acc = psum.tile([P, bags], F32, name=f"acc{i}_{m}")
+                    accs.append(acc[:])
+            else:
+                both = psum.tile([P, 2, bags], F32, name=f"acc{i}")
+                accs = [both[:, 0, :], both[:, 1, :]]
             for m in range(2):
-                acc = psum.tile([P, bags], F32, name=f"acc{i}_{m}")
                 cols = slice(m * P, (m + 1) * P)
                 nc.tensor.matmul_mx(
-                    acc[:],
+                    accs[m],
                     lhsT=w_codes[:, cols].bitcast(FP8X4),
                     lhsT_scale=w_scales[:, cols],
                     rhs=codes[:].bitcast(FP8X4),
@@ -120,9 +136,37 @@ def tile_attend_bag_kernel(tc, xT, w, offs, out):
                     start=True,
                     stop=True,
                 )
-                res = keep.tile([P, bags], F32, name=f"res{i}_{m}")
-                if m == 1 and i == len(BAGS) - 1:
-                    nc.vector.tensor_copy(res[:], acc[:])
-                else:
-                    nc.scalar.activation(res[:], acc[:], COPY)
-                nc.sync.dma_start(out[cols, starts[i] : starts[i] + bags], res[:])
+            g = slice(starts[i], starts[i] + bags)
+            if last:
+                res1 = keep.tile([P, bags], F32, name=f"res1_{i}")
+                nc.scalar.activation(res[:, 0, :], accs[0], COPY)
+                nc.vector.tensor_copy(res1[:], accs[1])
+                nc.scalar.dma_start(out[0:P, g], res[:, 0, :])
+                nc.sync.dma_start(out[P : 2 * P, g], res1[:])
+            else:
+                nc.scalar.activation(res[:], both[:], COPY)
+                nc.sync.dma_start(out_rows[:, :, g], res[:])
+
+        n = len(BAGS)
+        for h in range(2):
+            for k in range(len(LOADS[h])):
+                cast(h, k)
+        nc.scalar.activation(w_bf[:].rearrange("p (m t) -> p m t", t=4), w_raw[:].rearrange("p t m -> p m t"), COPY)
+        for i in range(n):
+            gather(0, i)
+            level1(0, i)
+        for i in range(n):
+            gather(1, i)
+            if (1, i) in GPSIMD:
+                level1(1, i)
+        quantise_w()
+        level1(1, 2)
+        level1(1, 3)
+        level2(0)
+        level2(1)
+        product(0)
+        level2(2)
+        product(1)
+        level2(3)
+        product(2)
+        product(3, last=True)

@@ -14,13 +14,10 @@ U8 = mybir.dt.uint8
 FP8X4 = mybir.dt.float8_e4m3fn_x4
 ADD = mybir.AluOpType.add
 COPY = mybir.ActivationFunctionType.Copy
-X = mybir.AxisListType.X
 
-LOADS = ((512, 512, 768, 256), (512, 512, 512, 256, 256))
-VECTOR_COLS = {(0, 2): 512, (0, 3): 160}
-BAGS = (128, 128, 128, 128)
-GPSIMD = {(0, 0), (0, 1), (0, 2), (0, 3), (1, 0), (1, 1)}
-REDUCED = ()
+FIRST_LOADS = (1024, 512, 512)
+FIRST_CASTS = (("scalar", 0, 512), ("vector", 512, 1024), ("vector", 1024, 1536), ("scalar", 1536, 1696), ("vector", 1696, 2048))
+SECOND_LOADS = (512, 512, 384, 384, 256)
 
 
 def tile_attend_bag_kernel(tc, xT, w, offs, out):
@@ -28,7 +25,6 @@ def tile_attend_bag_kernel(tc, xT, w, offs, out):
     x_rows = xT.rearrange("(p t) c -> p t c", t=4)
     w_rows = w.rearrange("(p t) m -> p t m", t=4)
     out_rows = out.rearrange("(m p) g -> p m g", m=2)
-    starts = [sum(BAGS[:i]) for i in range(len(BAGS))]
     with ExitStack() as ctx:
         keep = ctx.enter_context(tc.tile_pool(name="keep", bufs=1))
         psum = ctx.enter_context(tc.psum_pool(name="psum", bufs=1))
@@ -36,16 +32,20 @@ def tile_attend_bag_kernel(tc, xT, w, offs, out):
         offsets = keep.tile([P, G * K // 16], U16, name="offsets")
         pairs = [keep.tile([P, 2 * T], BF16, name=f"pair{h}") for h in range(2)]
 
-        raws = {}
-        for h in range(2):
-            c = 0
-            for k, cols in enumerate(LOADS[h]):
-                raw = keep.tile([P, 2, cols], F32, name=f"raw{h}_{k}")
-                nc.sync.dma_start(raw[:], x_rows[:, 2 * h : 2 * h + 2, c : c + cols])
-                raws[h, k] = (raw, c)
-                c += cols
-                if (h, k) == (0, 3):
-                    nc.sync.dma_start(offsets[:], offs)
+        first = keep.tile([P, 2, T], F32, name="first")
+        nc.sync.dma_start(first[:, 0, :], x_rows[:, 0, :])
+        c = 0
+        for cols in FIRST_LOADS:
+            nc.sync.dma_start(first[:, 1, c : c + cols], x_rows[:, 1, c : c + cols])
+            c += cols
+        nc.sync.dma_start(offsets[:], offs)
+        second = []
+        c = 0
+        for cols in SECOND_LOADS:
+            raw = keep.tile([P, 2, cols], F32, name=f"second{c}")
+            nc.sync.dma_start(raw[:], x_rows[:, 2:4, c : c + cols])
+            second.append((raw, c, cols))
+            c += cols
         w_raw = keep.tile([P, 4, M], F32, name="w_raw")
         nc.sync.dma_start(w_raw[:], w_rows)
 
@@ -54,55 +54,31 @@ def tile_attend_bag_kernel(tc, xT, w, offs, out):
         nc.vector.memset(warm[:], 0.0)
         nc.scalar.activation(warmed[:], warm[:], COPY)
 
-        def cast(h, k):
-            tile, c0 = raws[h, k]
-            cols = LOADS[h][k]
-            wide = pairs[h][:].rearrange("p (c t) -> p c t", t=2)
-            raw = tile[:].rearrange("p t c -> p c t")
-            split = cols - VECTOR_COLS.get((h, k), 0)
-            if split:
-                nc.scalar.activation(wide[:, c0 : c0 + split, :], raw[:, 0:split, :], COPY)
-            if split < cols:
-                nc.vector.tensor_copy(wide[:, c0 + split : c0 + cols, :], raw[:, split:cols, :])
-
-        sums = {}
-        e_bf = []
-        for i, bags in enumerate(BAGS):
-            if i not in REDUCED:
-                s = keep.tile([P, 2, bags, 4], F32, name=f"sums{i}")
-                sums[i] = s
-            e = keep.tile([P, bags * 4], BF16, name=f"e{i}", align_bytes=64)
-            e_bf.append(e)
+        sums = keep.tile([P, 2, G, 4], F32, name="sums")
+        e_bf = keep.tile([P, G * 4], BF16, name="e_bf", align_bytes=64)
+        codes = keep.tile([P, G], U32, name="codes", align_bytes=64)
+        scales = keep.tile([P, G], U8, name="scales", align_bytes=64)
         got = {}
 
-        def gather(h, i):
-            a = starts[i] * K // 16
-            b = a + BAGS[i] * K // 16
-            g = keep.tile([P, BAGS[i] * K], U32, name=f"got{h}_{i}")
+        def gather(h, g0, bags):
+            a = g0 * K // 16
+            b = a + bags * K // 16
+            g = keep.tile([P, bags * K], U32, name=f"got{h}_{g0}")
             nc.vector.tensor_copy(g[:], pairs[h][:].bitcast(U32).indirect(offsets[:, a:b]))
-            got[h, i] = g
+            got[h, g0] = g
 
-        def level1(h, i):
-            v = got[h, i][:].bitcast(BF16).rearrange("p (g e) -> p g e", e=8)
-            engine = nc.gpsimd if (h, i) in GPSIMD else nc.vector
-            engine.tensor_tensor(sums[i][:, h, :, :], v[:, :, 0:4], v[:, :, 4:8], ADD)
+        def level1(engine, h, g0, bags):
+            v = got[h, g0][:].bitcast(BF16).rearrange("p (g e) -> p g e", e=8)
+            engine.tensor_tensor(sums[:, h, g0 : g0 + bags, :], v[:, :, 0:4], v[:, :, 4:8], ADD)
 
-        def level2(i):
+        def level2(g0, bags):
+            s = sums[:, :, g0 : g0 + bags, :].rearrange("p h g e -> p g h e")
             nc.vector.tensor_tensor(
-                e_bf[i][:].rearrange("p (g h t) -> p g h t", h=2, t=2),
-                sums[i][:, :, :, 0:2].rearrange("p h g t -> p g h t"),
-                sums[i][:, :, :, 2:4].rearrange("p h g t -> p g h t"),
+                e_bf[:, 4 * g0 : 4 * (g0 + bags)].rearrange("p (g h t) -> p g h t", h=2, t=2),
+                s[:, :, :, 0:2],
+                s[:, :, :, 2:4],
                 ADD,
             )
-
-        def reduce(h, i):
-            with nc.allow_low_precision(reason="the engine adds in float32 and rounds the sum once"):
-                nc.vector.tensor_reduce(
-                    e_bf[i][:].rearrange("p (g h t) -> p g h t", h=2, t=2)[:, :, h, :],
-                    got[h, i][:].bitcast(BF16).rearrange("p (g j t) -> p g t j", j=4, t=2),
-                    axis=X,
-                    op=ADD,
-                )
 
         w_bf = keep.tile([P, M * 4], BF16, name="w_bf", align_bytes=64)
         w_codes = keep.tile([P, M], U32, name="w_codes", align_bytes=64)
@@ -111,19 +87,17 @@ def tile_attend_bag_kernel(tc, xT, w, offs, out):
         def quantise_w():
             nc.vector.quantize_mx(w_codes[:].bitcast(FP8X4), w_scales[:], w_bf[:])
 
-        def product(i, last=False):
-            bags = BAGS[i]
-            codes = keep.tile([P, bags], U32, name=f"codes{i}", align_bytes=64)
-            scales = keep.tile([P, bags], U8, name=f"scales{i}", align_bytes=64)
-            nc.vector.quantize_mx(codes[:].bitcast(FP8X4), scales[:], e_bf[i][:])
-            res = keep.tile([P, 2, bags], F32, name=f"res{i}")
-            accs = []
-            if last or bags > 256:
+        def product(g0, bags, last=False):
+            g = slice(g0, g0 + bags)
+            nc.vector.quantize_mx(codes[:, g].bitcast(FP8X4), scales[:, g], e_bf[:, 4 * g0 : 4 * (g0 + bags)])
+            res = keep.tile([P, 2, bags], F32, name=f"res{g0}")
+            if last:
+                accs = []
                 for m in range(2):
-                    acc = psum.tile([P, bags], F32, name=f"acc{i}_{m}")
+                    acc = psum.tile([P, bags], F32, name=f"acc{g0}_{m}")
                     accs.append(acc[:])
             else:
-                both = psum.tile([P, 2, bags], F32, name=f"acc{i}")
+                both = psum.tile([P, 2, bags], F32, name=f"acc{g0}")
                 accs = [both[:, 0, :], both[:, 1, :]]
             for m in range(2):
                 cols = slice(m * P, (m + 1) * P)
@@ -131,14 +105,13 @@ def tile_attend_bag_kernel(tc, xT, w, offs, out):
                     accs[m],
                     lhsT=w_codes[:, cols].bitcast(FP8X4),
                     lhsT_scale=w_scales[:, cols],
-                    rhs=codes[:].bitcast(FP8X4),
-                    rhs_scale=scales[:],
+                    rhs=codes[:, g].bitcast(FP8X4),
+                    rhs_scale=scales[:, g],
                     start=True,
                     stop=True,
                 )
-            g = slice(starts[i], starts[i] + bags)
             if last:
-                res1 = keep.tile([P, bags], F32, name=f"res1_{i}")
+                res1 = keep.tile([P, bags], F32, name=f"res1_{g0}")
                 nc.scalar.activation(res[:, 0, :], accs[0], COPY)
                 nc.vector.tensor_copy(res1[:], accs[1])
                 nc.scalar.dma_start(out[0:P, g], res[:, 0, :])
@@ -147,26 +120,31 @@ def tile_attend_bag_kernel(tc, xT, w, offs, out):
                 nc.scalar.activation(res[:], both[:], COPY)
                 nc.sync.dma_start(out_rows[:, :, g], res[:])
 
-        n = len(BAGS)
-        for h in range(2):
-            for k in range(len(LOADS[h])):
-                cast(h, k)
+        wide = [pair[:].rearrange("p (c t) -> p c t", t=2) for pair in pairs]
+        for engine, c0, c1 in FIRST_CASTS:
+            source = first[:, :, c0:c1].rearrange("p t c -> p c t")
+            if engine == "scalar":
+                nc.scalar.activation(wide[0][:, c0:c1, :], source, COPY)
+            else:
+                nc.vector.tensor_copy(wide[0][:, c0:c1, :], source)
+        for raw, c, cols in second:
+            nc.scalar.activation(wide[1][:, c : c + cols, :], raw[:].rearrange("p t c -> p c t"), COPY)
         nc.scalar.activation(w_bf[:].rearrange("p (m t) -> p m t", t=4), w_raw[:].rearrange("p t m -> p m t"), COPY)
-        for i in range(n):
-            gather(0, i)
-            level1(0, i)
-        for i in range(n):
-            gather(1, i)
-            if (1, i) in GPSIMD:
-                level1(1, i)
+        for g0, bags in ((0, 128), (128, 128), (256, 256)):
+            gather(0, g0, bags)
+            level1(nc.gpsimd, 0, g0, bags)
+        for g0 in range(0, G, 128):
+            gather(1, g0, 128)
+            if g0 < 256:
+                level1(nc.gpsimd, 1, g0, 128)
         quantise_w()
-        level1(1, 2)
-        level1(1, 3)
-        level2(0)
-        level2(1)
-        product(0)
-        level2(2)
-        product(1)
-        level2(3)
-        product(2)
-        product(3, last=True)
+        level1(nc.vector, 1, 256, 128)
+        level2(0, 128)
+        level1(nc.vector, 1, 384, 128)
+        product(0, 128)
+        level2(128, 128)
+        level2(256, 128)
+        product(128, 128)
+        level2(384, 128)
+        product(256, 128)
+        product(384, 128, last=True)

from contextlib import ExitStack

import concourse.mybir as mybir

D, T, G, K, M = 512, 2048, 512, 4, 256
P = 128
FLOPS = 2 * D * G * M

F32 = mybir.dt.float32
BF16 = mybir.dt.bfloat16
U32 = mybir.dt.uint32
U16 = mybir.dt.uint16
U8 = mybir.dt.uint8
FP8X4 = mybir.dt.float8_e4m3fn_x4
ADD = mybir.AluOpType.add
COPY = mybir.ActivationFunctionType.Copy

FIRST_LOADS = (1024, 512, 512)
FIRST_CASTS = (("scalar", 0, 512), ("vector", 512, 1024), ("vector", 1024, 1536), ("scalar", 1536, 1696), ("vector", 1696, 2048))
SECOND_LOADS = (512, 512, 384, 384, 256)


def tile_attend_bag_kernel(tc, xT, w, offs, out):
    nc = tc.nc
    x_rows = xT.rearrange("(p t) c -> p t c", t=4)
    w_rows = w.rearrange("(p t) m -> p t m", t=4)
    out_rows = out.rearrange("(m p) g -> p m g", m=2)
    with ExitStack() as ctx:
        keep = ctx.enter_context(tc.tile_pool(name="keep", bufs=1))
        psum = ctx.enter_context(tc.psum_pool(name="psum", bufs=1))

        offsets = keep.tile([P, G * K // 16], U16, name="offsets")
        pairs = [keep.tile([P, 2 * T], BF16, name=f"pair{h}") for h in range(2)]

        first = keep.tile([P, 2, T], F32, name="first")
        nc.sync.dma_start(first[:, 0, :], x_rows[:, 0, :])
        c = 0
        for cols in FIRST_LOADS:
            nc.sync.dma_start(first[:, 1, c : c + cols], x_rows[:, 1, c : c + cols])
            c += cols
        nc.sync.dma_start(offsets[:], offs)
        second = []
        c = 0
        for cols in SECOND_LOADS:
            raw = keep.tile([P, 2, cols], F32, name=f"second{c}")
            nc.sync.dma_start(raw[:], x_rows[:, 2:4, c : c + cols])
            second.append((raw, c, cols))
            c += cols
        w_raw = keep.tile([P, 4, M], F32, name="w_raw")
        nc.sync.dma_start(w_raw[:], w_rows)

        warm = keep.tile([P, 1], F32, name="warm")
        warmed = keep.tile([P, 1], F32, name="warmed")
        nc.vector.memset(warm[:], 0.0)
        nc.scalar.activation(warmed[:], warm[:], COPY)

        sums = keep.tile([P, 2, G, 4], F32, name="sums")
        e_bf = keep.tile([P, G * 4], BF16, name="e_bf", align_bytes=64)
        codes = keep.tile([P, G], U32, name="codes", align_bytes=64)
        scales = keep.tile([P, G], U8, name="scales", align_bytes=64)
        got = {}

        def gather(h, g0, bags):
            a = g0 * K // 16
            b = a + bags * K // 16
            g = keep.tile([P, bags * K], U32, name=f"got{h}_{g0}")
            nc.vector.tensor_copy(g[:], pairs[h][:].bitcast(U32).indirect(offsets[:, a:b]))
            got[h, g0] = g

        def level1(engine, h, g0, bags):
            v = got[h, g0][:].bitcast(BF16).rearrange("p (g e) -> p g e", e=8)
            engine.tensor_tensor(sums[:, h, g0 : g0 + bags, :], v[:, :, 0:4], v[:, :, 4:8], ADD)

        def level2(g0, bags):
            s = sums[:, :, g0 : g0 + bags, :].rearrange("p h g e -> p g h e")
            nc.vector.tensor_tensor(
                e_bf[:, 4 * g0 : 4 * (g0 + bags)].rearrange("p (g h t) -> p g h t", h=2, t=2),
                s[:, :, :, 0:2],
                s[:, :, :, 2:4],
                ADD,
            )

        w_bf = keep.tile([P, M * 4], BF16, name="w_bf", align_bytes=64)
        w_codes = keep.tile([P, M], U32, name="w_codes", align_bytes=64)
        w_scales = keep.tile([P, M], U8, name="w_scales", align_bytes=64)

        def quantise_w():
            nc.vector.quantize_mx(w_codes[:].bitcast(FP8X4), w_scales[:], w_bf[:])

        def product(g0, bags, last=False):
            g = slice(g0, g0 + bags)
            nc.vector.quantize_mx(codes[:, g].bitcast(FP8X4), scales[:, g], e_bf[:, 4 * g0 : 4 * (g0 + bags)])
            res = keep.tile([P, 2, bags], F32, name=f"res{g0}")
            if last:
                accs = []
                for m in range(2):
                    acc = psum.tile([P, bags], F32, name=f"acc{g0}_{m}")
                    accs.append(acc[:])
            else:
                both = psum.tile([P, 2, bags], F32, name=f"acc{g0}")
                accs = [both[:, 0, :], both[:, 1, :]]
            for m in range(2):
                cols = slice(m * P, (m + 1) * P)
                nc.tensor.matmul_mx(
                    accs[m],
                    lhsT=w_codes[:, cols].bitcast(FP8X4),
                    lhsT_scale=w_scales[:, cols],
                    rhs=codes[:, g].bitcast(FP8X4),
                    rhs_scale=scales[:, g],
                    start=True,
                    stop=True,
                )
            if last:
                res1 = keep.tile([P, bags], F32, name=f"res1_{g0}")
                nc.scalar.activation(res[:, 0, :], accs[0], COPY)
                nc.vector.tensor_copy(res1[:], accs[1])
                nc.scalar.dma_start(out[0:P, g], res[:, 0, :])
                nc.sync.dma_start(out[P : 2 * P, g], res1[:])
            else:
                nc.scalar.activation(res[:], both[:], COPY)
                nc.sync.dma_start(out_rows[:, :, g], res[:])

        wide = [pair[:].rearrange("p (c t) -> p c t", t=2) for pair in pairs]
        for engine, c0, c1 in FIRST_CASTS:
            source = first[:, :, c0:c1].rearrange("p t c -> p c t")
            if engine == "scalar":
                nc.scalar.activation(wide[0][:, c0:c1, :], source, COPY)
            else:
                nc.vector.tensor_copy(wide[0][:, c0:c1, :], source)
        for raw, c, cols in second:
            nc.scalar.activation(wide[1][:, c : c + cols, :], raw[:].rearrange("p t c -> p c t"), COPY)
        nc.scalar.activation(w_bf[:].rearrange("p (m t) -> p m t", t=4), w_raw[:].rearrange("p t m -> p m t"), COPY)
        for g0, bags in ((0, 128), (128, 128), (256, 256)):
            gather(0, g0, bags)
            level1(nc.gpsimd, 0, g0, bags)
        for g0 in range(0, G, 128):
            gather(1, g0, 128)
            if g0 < 256:
                level1(nc.gpsimd, 1, g0, 128)
        quantise_w()
        level1(nc.vector, 1, 256, 128)
        level2(0, 128)
        level1(nc.vector, 1, 384, 128)
        product(0, 128)
        level2(128, 128)
        level2(256, 128)
        product(128, 128)
        level2(384, 128)
        product(256, 128)
        product(384, 128, last=True)
